import numpy as np
import ml_dtypes


def mxq(x, axis, fmt="e4m3"):
    dtype, down = {"e4m3": (ml_dtypes.float8_e4m3fn, 7), "e5m2": (ml_dtypes.float8_e5m2, 14)}[fmt]
    v = np.moveaxis(np.asarray(x, np.float32).astype(ml_dtypes.bfloat16).astype(np.float64), axis, -1)
    blocks = v.reshape(v.shape[:-1] + (-1, 32))
    amax = np.abs(blocks).max(-1, keepdims=True)
    byte = np.maximum(np.where(amax > 0, np.frexp(amax)[1] - 1 + 127, 0) - down, 1)
    scale = np.exp2(byte - 127.0)
    codes = (blocks / scale).astype(np.float32).astype(dtype).astype(np.float64)
    return np.moveaxis((codes * scale).reshape(v.shape), -1, axis)


WIDE = False


def mx_kscale(k):
    if not WIDE:
        return np.ones(k)
    levels = np.array([10, -10, 5, -5, 0])
    if k % 512:
        return np.exp2(np.random.permutation(np.resize(levels, k // 32))).repeat(32)
    a = np.empty((k // 512, 16))
    for p in range(k // 512):
        a[p, :8] = np.random.permutation(np.resize(levels, 8))
        for g in range(8):
            far = levels[np.abs(levels - a[p, g]) >= 10]
            a[p, g + 8] = far[np.random.randint(len(far))]
    return np.exp2(a.ravel()).repeat(32)


def f64(x):
    return np.asarray(x).astype(np.float64)


def striped(idx):
    return np.tile(np.asarray(idx).reshape(-1, 16).T, (8, 1)).astype(np.uint16)


def unstriped(offs):
    return offs[:16].T.reshape(-1).astype(np.int64)


E2M1 = np.array([0.0, 0.5, 1.0, 1.5, 2.0, 3.0, 4.0, 6.0, -0.0, -0.5, -1.0, -1.5, -2.0, -3.0, -4.0, -6.0])


def pack_weight(w, fmt):
    k, n = w.shape
    w = f64(np.asarray(w, np.float32).astype(ml_dtypes.bfloat16)).reshape(k // 32, 32, n)
    amax = np.abs(w).max(1)
    if fmt == "e4m3":
        byte = np.frexp(amax)[1] - 1 + 127 - 7
    else:
        mant, ex = np.frexp(amax / 6.0)
        byte = np.where(mant > 0.5, ex, ex - 1) + 127
    byte = np.clip(np.where(amax > 0, byte, 1), 1, 254)
    scaled = (w * np.exp2(127.0 - byte)[:, None, :]).reshape(k, n).astype(np.float32)
    by_word = np.ascontiguousarray(scaled.reshape(k // 512, 128, 4, n).transpose(0, 1, 3, 2))
    if fmt == "e4m3":
        words = by_word.astype(ml_dtypes.float8_e4m3fn).view(np.uint8)
    else:
        c = by_word.astype(ml_dtypes.float4_e2m1fn).view(np.uint8) & 0xF
        words = (c[..., 0::2] | (c[..., 1::2] << 4)).reshape(k // 512, 128, 2 * n)
    return np.ascontiguousarray(words), np.ascontiguousarray(byte.astype(np.uint8).reshape(k // 512, 16, n))


def unpack_weight(words, scales, fmt):
    g, _, n = scales.shape
    words = np.ascontiguousarray(words).reshape(g, 128, n, -1)
    if fmt == "e4m3":
        vals = words.view(ml_dtypes.float8_e4m3fn).astype(np.float64)
    else:
        nib = np.empty((g, 128, n, 4), np.uint8)
        nib[..., 0::2] = words & 0xF
        nib[..., 1::2] = words >> 4
        vals = E2M1[nib]
    vals = vals * np.repeat(np.exp2(scales.astype(np.float64) - 127.0), 8, axis=1)[..., None]
    return vals.transpose(0, 1, 3, 2).reshape(g * 512, n)


D, T, I, J, U, E, M = 512, 2048, 512, 512, 1024, 512, 1024


def setup_inputs():
    n = np.random.standard_normal
    idx = np.random.permutation(T)[:I]
    idx2 = np.random.permutation(U)[:J]
    idx3 = np.random.permutation(U)[:J]
    idx4 = np.random.permutation(M)[:J]
    fd = mx_kscale(D)
    fi = mx_kscale(I)
    ti = np.ones(T)
    ti[idx] = fi
    keysp = pack_weight(n((D, T)) / fd[:, None], "e4m3")
    return {
        "keys_words": keysp[0],
        "keys_scales": keysp[1],
        "notes": (n((D, U)) * 1.0 / np.sqrt(D) * fd[:, None]).astype(np.float32),
        "rowf": (np.random.uniform(0.02, 0.08, (I, 1)) * fi[:, None]).astype(np.float32),
        "vals": (n((E, T)) / ti).astype(np.float32),
        "old": (1.0 * n((E, M))).astype(np.float32),
        "offs": striped(idx),
        "offs2": striped(idx2),
        "offs3": striped(idx3),
        "offs4": striped(idx4),
    }


def reference(keys_words, keys_scales, notes, rowf, vals, old, offs, offs2, offs3, offs4):
    idx = unstriped(offs)
    idx2 = unstriped(offs2)
    idx3 = unstriped(offs3)
    idx4 = unstriped(offs4)
    keysu = unpack_weight(keys_words, keys_scales, "e4m3")
    keysidxg = keysu[:, idx]
    notesq = mxq(f64(notes), 0, "e4m3")
    g1 = keysidxg.T @ notesq
    g9 = g1[:, idx2] - g1[:, idx3]
    g0 = np.maximum(g9, 0.0)
    gr1 = g0 * f64(rowf)
    vt1 = f64(vals)[:, idx].T
    vt1q = mxq(vt1, 0, "e4m3")
    gr1q = mxq(gr1, 0, "e4m3")
    o = vt1q.T @ gr1q
    of = np.zeros((E, M))
    of[:, idx4] = o
    y = f64(old) + of
    return y

@@ -1,0 +1,214 @@
+from contextlib import ExitStack
+
+import concourse.mybir as mybir
+from concourse.masks import make_identity
+
+D, T, I, J, U, E, M = 512, 2048, 512, 512, 1024, 512, 1024
+FLOPS = 2 * D * I * U + 2 * I * E * J
+
+F32 = mybir.dt.float32
+BF16 = mybir.dt.bfloat16
+U32 = mybir.dt.uint32
+I32 = mybir.dt.int32
+U16 = mybir.dt.uint16
+U8 = mybir.dt.uint8
+FP8X4 = mybir.dt.float8_e4m3fn_x4
+ALU = mybir.AluOpType
+COPY = mybir.ActivationFunctionType.Copy
+
+P = 128
+PACK = 4
+BANK = 512
+NOTE_CHUNKS = ((0, 512), (512, 768), (768, 1024))
+SHARE = 256
+
+
+def tile_attend_tab_looked_put_kernel(tc, keys_words, keys_scales, notes, rowf, vals, old, offs, offs2, offs3, offs4, out):
+    nc = tc.nc
+    with ExitStack() as ctx:
+        sb = ctx.enter_context(tc.tile_pool(name="sb", bufs=1))
+        ps = ctx.enter_context(tc.psum_pool(name="ps", bufs=1))
+
+        def tile(shape, dtype, name, tag=None):
+            return sb.tile(shape, dtype, name=name, tag=tag or name, align_bytes=64)
+
+        def bank(shape, name):
+            return ps.tile(shape, F32, name=name, tag="bank", bufs=8)
+
+        lst1 = tile([P, I // 16], U16, "lst1")
+        lst2 = tile([P, J // 16], U16, "lst2")
+        lst3 = tile([P, J // 16], U16, "lst3")
+        lst4 = tile([P, J // 16], U16, "lst4")
+        kpool_w = tile([P, T], U32, "kpool_w")
+        kpool_s = tile([P, T], U8, "kpool_s")
+        raw = [tile([P, PACK, b - a], F32, "raw%d" % a) for a, b in NOTE_CHUNKS]
+        rf = tile([P, PACK], F32, "rf")
+        vpool = [tile([P, T], F32, "vpool%d" % e) for e in range(4)]
+        prev = [tile([P, M], F32, "prev%d" % e) for e in range(4)]
+        win = [tile([P, M], F32, "win%d" % e) for e in range(4)]
+        ident = tile([P, P], F32, "ident")
+
+        nc.gpsimd.memset(kpool_s[:].bitcast(I32), 0)
+        notes_p = notes.rearrange("(p t) u -> p t u", t=PACK)
+
+        def load_notes(c):
+            a, b = NOTE_CHUNKS[c]
+            nc.sync.dma_start(raw[c][:], notes_p[:, :, a:b])
+
+        nc.sync.dma_start(lst1[:], offs)
+        load_notes(0)
+        for q in range(4):
+            nc.sync.dma_start(kpool_s[32 * q : 32 * q + 4, :].bitcast(I32), keys_scales[0][4 * q : 4 * q + 4, :].bitcast(I32))
+        nc.sync.dma_start(kpool_w[:].bitcast(I32), keys_words[0].rearrange("p n t -> p (n t)").bitcast(I32))
+        load_notes(1)
+        load_notes(2)
+        nc.sync.dma_start(lst3[:], offs3)
+        nc.sync.dma_start(lst2[:], offs2)
+        nc.sync.dma_start(rf[:], rowf.rearrange("(p r) o -> p (r o)", r=PACK))
+        for e in range(4):
+            nc.sync.dma_start(vpool[e][:], vals[e * P : (e + 1) * P, :])
+        nc.sync.dma_start(lst4[:], offs4)
+        for e in (1, 0, 2, 3):
+            nc.sync.dma_start(prev[e][:], old[e * P : (e + 1) * P, :])
+        for e in range(4):
+            nc.vector.memset(win[e][:], 0.0)
+        make_identity(nc, ident[:])
+
+        nw = tile([P, U], U32, "nw")
+        ns = tile([P, U], U8, "ns")
+        nb = [tile([P, b - a, PACK], BF16, "nb%d" % a) for a, b in NOTE_CHUNKS]
+
+        def weave_notes(on_vector, c, a, b):
+            base = NOTE_CHUNKS[c][0]
+            src = raw[c][:, :, a - base : b - base].rearrange("p t (c i) -> p c t i", i=4)
+            dst = nb[c][:, a - base : b - base, :].rearrange("p (c i) t -> p c t i", i=4)
+            if on_vector:
+                nc.vector.tensor_copy(dst, src)
+            else:
+                nc.scalar.activation(dst, src, COPY)
+
+        def quant_notes(c):
+            a, b = NOTE_CHUNKS[c]
+            nc.vector.quantize_mx(out=nw[:, a:b].bitcast(FP8X4), scales=ns[:, a:b], in_=nb[c][:].rearrange("p u t -> p (u t)"))
+
+        weave_notes(True, 0, 0, 320)
+        weave_notes(False, 0, 320, 512)
+        quant_notes(0)
+        kw = tile([P, I], U32, "kw")
+        ks = tile([P, I], U8, "ks")
+        nc.vector.tensor_copy(ks[:].rearrange("p (r s) -> p s r", r=PACK), kpool_s[:].indirect(lst1[:]))
+        nc.vector.tensor_copy(kw[:].rearrange("p (r s) -> p s r", r=PACK), kpool_w[:].indirect(lst1[:]))
+        weave_notes(True, 1, 512, 768)
+        weave_notes(True, 2, 768, 1024)
+        quant_notes(1)
+        quant_notes(2)
+
+        g1 = [tile([P, U], F32, "g1_%d" % r) for r in range(PACK)]
+        low = [tile([P, J], F32, "low%d" % r) for r in range(PACK)]
+        g9 = [tile([P, J], F32, "g9_%d" % r) for r in range(PACK)]
+        grp = tile([P, PACK, J], BF16, "grp")
+        for r in range(PACK):
+            rows = slice(r * P, (r + 1) * P)
+            for a, b in NOTE_CHUNKS if r == 0 else ((0, BANK), (BANK, U)):
+                acc = bank([P, b - a], "acc")
+                nc.tensor.matmul_mx(out=acc[:], lhsT=kw[:, rows].bitcast(FP8X4), lhsT_scale=ks[:, rows],
+                                    rhs=nw[:, a:b].bitcast(FP8X4), rhs_scale=ns[:, a:b], start=True, stop=True)
+                if b == U:
+                    nc.vector.tensor_copy(g1[r][:, a:b], acc[:])
+                else:
+                    nc.scalar.copy(g1[r][:, a:b], acc[:])
+        for r in range(PACK):
+            nc.scalar.activation(low[r][:], g1[r][:].indirect(lst3[:]), COPY)
+
+        def scale_rows(r):
+            nc.vector.tensor_scalar(grp[:, r, :], g9[r][:], 0.0, rf[:, r : r + 1], ALU.max, ALU.mult)
+
+        for r in range(PACK):
+            nc.vector.tensor_tensor(g9[r][:], g1[r][:].indirect(lst2[:]), low[r][:], ALU.subtract)
+            if r > 0:
+                scale_rows(r - 1)
+        scale_rows(PACK - 1)
+        gb = tile([P, J, PACK], BF16, "gb")
+        halves = (slice(0, J // 2), slice(J // 2, J))
+        for js in halves:
+            nc.vector.tensor_copy(gb[:, js, :].rearrange("p (c i) t -> p c t i", i=4), grp[:, :, js].rearrange("p t (c i) -> p c t i", i=4))
+
+        vg = {}
+        turned = {}
+
+        def gather_vals(e):
+            vg[e] = tile([P, I], BF16, "vg%d" % e)
+            nc.scalar.activation(vg[e][:], vpool[e][:].indirect(lst1[:]), COPY)
+            pairs = vg[e][:].bitcast(F32)
+            turned[e] = bank([P, 2, P], "turned")
+            for u in range(2):
+                nc.tensor.transpose(turned[e][:, u, :], pairs[:, u : 2 * P : 2], ident[:])
+
+        def quant_vals(first, wtag, btag):
+            vb = tile([P, 2 * P, PACK], BF16, "vb%d" % first, btag)
+            for k in range(2):
+                nc.scalar.copy(vb[:, k * P : (k + 1) * P, :].rearrange("p e t -> p (e t)").bitcast(F32).rearrange("p (e u) -> p e u", u=2),
+                               turned[first + k][:].rearrange("p u e -> p e u"))
+            vw = tile([P, 2 * P], U32, "vw%d" % first, wtag)
+            vs = tile([P, 2 * P], U8, "vs%d" % first)
+            nc.vector.quantize_mx(out=vw[:].bitcast(FP8X4), scales=vs[:], in_=vb[:].rearrange("p e t -> p (e t)"))
+            return vw, vs
+
+        gather_vals(0)
+        gather_vals(1)
+        gather_vals(2)
+        vq = [quant_vals(0, "grp", "vpool2")]
+        gw = tile([P, J], U32, "gw", "vpool2")
+        gs = tile([P, J], U8, "gs")
+        for js in halves:
+            nc.vector.quantize_mx(out=gw[:, js].bitcast(FP8X4), scales=gs[:, js], in_=gb[:, js, :].rearrange("p j t -> p (j t)"))
+        gather_vals(3)
+        vq.append(quant_vals(2, None, "vpool3"))
+
+        def product(e, pieces):
+            vw, vs = vq[e // 2]
+            cols = slice((e % 2) * P, (e % 2 + 1) * P)
+            prod = bank([P, J], "prod")
+            for js in pieces:
+                nc.tensor.matmul_mx(out=prod[:, js], lhsT=vw[:, cols].bitcast(FP8X4), lhsT_scale=vs[:, cols],
+                                    rhs=gw[:, js].bitcast(FP8X4), rhs_scale=gs[:, js], start=True, stop=True)
+            return prod
+
+        def fetch(on_vector, prod, a, b, name, tag):
+            res = tile([P, b - a], F32, name, tag)
+            if on_vector:
+                nc.vector.tensor_copy(res[:], prod[:, a:b])
+            else:
+                nc.scalar.copy(res[:], prod[:, a:b])
+            return res
+
+        def put(on_vector, e, values, a, b):
+            dst = win[e][:].indirect(lst4[:, a // 16 : b // 16])
+            if on_vector:
+                nc.vector.tensor_copy(dst, values)
+            else:
+                nc.scalar.activation(dst, values, COPY)
+
+        def finish(e, a, b):
+            nc.vector.tensor_tensor(prev[e][:, a:b], prev[e][:, a:b], win[e][:, a:b], ALU.add)
+            nc.sync.dma_start(out[e * P : (e + 1) * P, a:b], prev[e][:, a:b])
+
+        half = J // 2
+        res1 = fetch(True, product(1, halves), 0, J, "res1", None)
+        put(True, 1, res1[:], 0, J)
+        res0 = fetch(False, product(0, halves), 0, J, "res0", "vg3")
+        put(False, 0, res0[:, :half], 0, half)
+        put(False, 0, res0[:, half:], half, J)
+        prod2 = product(2, (slice(0, J),))
+        res2s = fetch(False, prod2, 0, SHARE, "res2s", None)
+        put(False, 2, res2s[:], 0, SHARE)
+        res3 = fetch(False, product(3, (slice(0, J),)), 0, J, "res3", "res2s")
+        put(False, 3, res3[:, :half], 0, half)
+        put(False, 3, res3[:, half:], half, J)
+        finish(1, 0, M)
+        finish(0, 0, M)
+        res2v = fetch(True, prod2, SHARE, J, "res2v", None)
+        put(True, 2, res2v[:], SHARE, J)
+        finish(2, 0, M)
+        finish(3, 0, M // 2)
+        finish(3, M // 2, M)

@@ -20,7 +20,7 @@ P = 128
 PACK = 4
 BANK = 512
 NOTE_CHUNKS = ((0, 512), (512, 768), (768, 1024))
-SHARE = 256
+SHARE = 224
 
 
 def tile_attend_tab_looked_put_kernel(tc, keys_words, keys_scales, notes, rowf, vals, old, offs, offs2, offs3, offs4, out):
@@ -144,10 +144,10 @@ def tile_attend_tab_looked_put_kernel(tc, keys_words, keys_scales, notes, rowf, 
             for u in range(2):
                 nc.tensor.transpose(turned[e][:, u, :], pairs[:, u : 2 * P : 2], ident[:])
 
-        def quant_vals(first, wtag, btag):
+        def quant_vals(first, wtag, btag, copy):
             vb = tile([P, 2 * P, PACK], BF16, "vb%d" % first, btag)
             for k in range(2):
-                nc.scalar.copy(vb[:, k * P : (k + 1) * P, :].rearrange("p e t -> p (e t)").bitcast(F32).rearrange("p (e u) -> p e u", u=2),
+                copy(vb[:, k * P : (k + 1) * P, :].rearrange("p e t -> p (e t)").bitcast(F32).rearrange("p (e u) -> p e u", u=2),
                                turned[first + k][:].rearrange("p u e -> p e u"))
             vw = tile([P, 2 * P], U32, "vw%d" % first, wtag)
             vs = tile([P, 2 * P], U8, "vs%d" % first)
@@ -157,13 +157,13 @@ def tile_attend_tab_looked_put_kernel(tc, keys_words, keys_scales, notes, rowf, 
         gather_vals(0)
         gather_vals(1)
         gather_vals(2)
-        vq = [quant_vals(0, "grp", "vpool2")]
-        gw = tile([P, J], U32, "gw", "vpool2")
+        gather_vals(3)
+        vq = [quant_vals(0, None, "grp", nc.vector.tensor_copy)]
+        gw = tile([P, J], U32, "gw")
         gs = tile([P, J], U8, "gs")
         for js in halves:
             nc.vector.quantize_mx(out=gw[:, js].bitcast(FP8X4), scales=gs[:, js], in_=gb[:, js, :].rearrange("p j t -> p (j t)"))
-        gather_vals(3)
-        vq.append(quant_vals(2, None, "vpool3"))
+        vq.append(quant_vals(2, "gb", "vpool3", nc.scalar.copy))
 
         def product(e, pieces):
             vw, vs = vq[e // 2]
@@ -189,14 +189,17 @@ def tile_attend_tab_looked_put_kernel(tc, keys_words, keys_scales, notes, rowf, 
             else:
                 nc.scalar.activation(dst, values, COPY)
 
-        def finish(e, a, b):
-            nc.vector.tensor_tensor(prev[e][:, a:b], prev[e][:, a:b], win[e][:, a:b], ALU.add)
-            nc.sync.dma_start(out[e * P : (e + 1) * P, a:b], prev[e][:, a:b])
+        def finish(e, tag, pieces):
+            total = tile([P, M], F32, "total%d" % e, tag)
+            for ms in pieces:
+                nc.vector.tensor_tensor(total[:, ms], prev[e][:, ms], win[e][:, ms], ALU.add)
+                nc.sync.dma_start(out[e * P : (e + 1) * P, ms], total[:, ms])
 
         half = J // 2
-        res1 = fetch(True, product(1, halves), 0, J, "res1", None)
+        whole = (slice(0, M),)
+        res0 = fetch(False, product(0, halves), 0, J, "res0", None)
+        res1 = fetch(True, product(1, halves), 0, J, "res1", "vpool3")
         put(True, 1, res1[:], 0, J)
-        res0 = fetch(False, product(0, halves), 0, J, "res0", "vg3")
         put(False, 0, res0[:, :half], 0, half)
         put(False, 0, res0[:, half:], half, J)
         prod2 = product(2, (slice(0, J),))
@@ -205,10 +208,9 @@ def tile_attend_tab_looked_put_kernel(tc, keys_words, keys_scales, notes, rowf, 
         res3 = fetch(False, product(3, (slice(0, J),)), 0, J, "res3", "res2s")
         put(False, 3, res3[:, :half], 0, half)
         put(False, 3, res3[:, half:], half, J)
-        finish(1, 0, M)
-        finish(0, 0, M)
-        res2v = fetch(True, prod2, SHARE, J, "res2v", None)
+        finish(1, None, whole)
+        finish(0, "vpool3", whole)
+        res2v = fetch(True, prod2, SHARE, J, "res2v", "prev1")
         put(True, 2, res2v[:], SHARE, J)
-        finish(2, 0, M)
-        finish(3, 0, M // 2)
-        finish(3, M // 2, M)
+        finish(2, None, (slice(0, M // 2), slice(M // 2, M)))
+        finish(3, "prev1", (slice(0, M // 2), slice(M // 2, 3 * M // 4), slice(3 * M // 4, M)))

from contextlib import ExitStack

import concourse.mybir as mybir
from concourse.masks import make_identity

D, T, I, J, U, E, M = 512, 2048, 512, 512, 1024, 512, 1024
FLOPS = 2 * D * I * U + 2 * I * E * J

F32 = mybir.dt.float32
BF16 = mybir.dt.bfloat16
U32 = mybir.dt.uint32
I32 = mybir.dt.int32
U16 = mybir.dt.uint16
U8 = mybir.dt.uint8
FP8X4 = mybir.dt.float8_e4m3fn_x4
ALU = mybir.AluOpType
COPY = mybir.ActivationFunctionType.Copy

P = 128
PACK = 4
BANK = 512
NOTE_CHUNKS = ((0, 512), (512, 768), (768, 1024))
SHARE = 224


def tile_attend_tab_looked_put_kernel(tc, keys_words, keys_scales, notes, rowf, vals, old, offs, offs2, offs3, offs4, out):
    nc = tc.nc
    with ExitStack() as ctx:
        sb = ctx.enter_context(tc.tile_pool(name="sb", bufs=1))
        ps = ctx.enter_context(tc.psum_pool(name="ps", bufs=1))

        def tile(shape, dtype, name, tag=None):
            return sb.tile(shape, dtype, name=name, tag=tag or name, align_bytes=64)

        def bank(shape, name):
            return ps.tile(shape, F32, name=name, tag="bank", bufs=8)

        lst1 = tile([P, I // 16], U16, "lst1")
        lst2 = tile([P, J // 16], U16, "lst2")
        lst3 = tile([P, J // 16], U16, "lst3")
        lst4 = tile([P, J // 16], U16, "lst4")
        kpool_w = tile([P, T], U32, "kpool_w")
        kpool_s = tile([P, T], U8, "kpool_s")
        raw = [tile([P, PACK, b - a], F32, "raw%d" % a) for a, b in NOTE_CHUNKS]
        rf = tile([P, PACK], F32, "rf")
        vpool = [tile([P, T], F32, "vpool%d" % e) for e in range(4)]
        prev = [tile([P, M], F32, "prev%d" % e) for e in range(4)]
        win = [tile([P, M], F32, "win%d" % e) for e in range(4)]
        ident = tile([P, P], F32, "ident")

        nc.gpsimd.memset(kpool_s[:].bitcast(I32), 0)
        notes_p = notes.rearrange("(p t) u -> p t u", t=PACK)

        def load_notes(c):
            a, b = NOTE_CHUNKS[c]
            nc.sync.dma_start(raw[c][:], notes_p[:, :, a:b])

        nc.sync.dma_start(lst1[:], offs)
        load_notes(0)
        for q in range(4):
            nc.sync.dma_start(kpool_s[32 * q : 32 * q + 4, :].bitcast(I32), keys_scales[0][4 * q : 4 * q + 4, :].bitcast(I32))
        nc.sync.dma_start(kpool_w[:].bitcast(I32), keys_words[0].rearrange("p n t -> p (n t)").bitcast(I32))
        load_notes(1)
        load_notes(2)
        nc.sync.dma_start(lst3[:], offs3)
        nc.sync.dma_start(lst2[:], offs2)
        nc.sync.dma_start(rf[:], rowf.rearrange("(p r) o -> p (r o)", r=PACK))
        for e in range(4):
            nc.sync.dma_start(vpool[e][:], vals[e * P : (e + 1) * P, :])
        nc.sync.dma_start(lst4[:], offs4)
        for e in (1, 0, 2, 3):
            nc.sync.dma_start(prev[e][:], old[e * P : (e + 1) * P, :])
        for e in range(4):
            nc.vector.memset(win[e][:], 0.0)
        make_identity(nc, ident[:])

        nw = tile([P, U], U32, "nw")
        ns = tile([P, U], U8, "ns")
        nb = [tile([P, b - a, PACK], BF16, "nb%d" % a) for a, b in NOTE_CHUNKS]

        def weave_notes(on_vector, c, a, b):
            base = NOTE_CHUNKS[c][0]
            src = raw[c][:, :, a - base : b - base].rearrange("p t (c i) -> p c t i", i=4)
            dst = nb[c][:, a - base : b - base, :].rearrange("p (c i) t -> p c t i", i=4)
            if on_vector:
                nc.vector.tensor_copy(dst, src)
            else:
                nc.scalar.activation(dst, src, COPY)

        def quant_notes(c):
            a, b = NOTE_CHUNKS[c]
            nc.vector.quantize_mx(out=nw[:, a:b].bitcast(FP8X4), scales=ns[:, a:b], in_=nb[c][:].rearrange("p u t -> p (u t)"))

        weave_notes(True, 0, 0, 320)
        weave_notes(False, 0, 320, 512)
        quant_notes(0)
        kw = tile([P, I], U32, "kw")
        ks = tile([P, I], U8, "ks")
        nc.vector.tensor_copy(ks[:].rearrange("p (r s) -> p s r", r=PACK), kpool_s[:].indirect(lst1[:]))
        nc.vector.tensor_copy(kw[:].rearrange("p (r s) -> p s r", r=PACK), kpool_w[:].indirect(lst1[:]))
        weave_notes(True, 1, 512, 768)
        weave_notes(True, 2, 768, 1024)
        quant_notes(1)
        quant_notes(2)

        g1 = [tile([P, U], F32, "g1_%d" % r) for r in range(PACK)]
        low = [tile([P, J], F32, "low%d" % r) for r in range(PACK)]
        g9 = [tile([P, J], F32, "g9_%d" % r) for r in range(PACK)]
        grp = tile([P, PACK, J], BF16, "grp")
        for r in range(PACK):
            rows = slice(r * P, (r + 1) * P)
            for a, b in NOTE_CHUNKS if r == 0 else ((0, BANK), (BANK, U)):
                acc = bank([P, b - a], "acc")
                nc.tensor.matmul_mx(out=acc[:], lhsT=kw[:, rows].bitcast(FP8X4), lhsT_scale=ks[:, rows],
                                    rhs=nw[:, a:b].bitcast(FP8X4), rhs_scale=ns[:, a:b], start=True, stop=True)
                if b == U:
                    nc.vector.tensor_copy(g1[r][:, a:b], acc[:])
                else:
                    nc.scalar.copy(g1[r][:, a:b], acc[:])
        for r in range(PACK):
            nc.scalar.activation(low[r][:], g1[r][:].indirect(lst3[:]), COPY)

        def scale_rows(r):
            nc.vector.tensor_scalar(grp[:, r, :], g9[r][:], 0.0, rf[:, r : r + 1], ALU.max, ALU.mult)

        for r in range(PACK):
            nc.vector.tensor_tensor(g9[r][:], g1[r][:].indirect(lst2[:]), low[r][:], ALU.subtract)
            if r > 0:
                scale_rows(r - 1)
        scale_rows(PACK - 1)
        gb = tile([P, J, PACK], BF16, "gb")
        halves = (slice(0, J // 2), slice(J // 2, J))
        for js in halves:
            nc.vector.tensor_copy(gb[:, js, :].rearrange("p (c i) t -> p c t i", i=4), grp[:, :, js].rearrange("p t (c i) -> p c t i", i=4))

        vg = {}
        turned = {}

        def gather_vals(e):
            vg[e] = tile([P, I], BF16, "vg%d" % e)
            nc.scalar.activation(vg[e][:], vpool[e][:].indirect(lst1[:]), COPY)
            pairs = vg[e][:].bitcast(F32)
            turned[e] = bank([P, 2, P], "turned")
            for u in range(2):
                nc.tensor.transpose(turned[e][:, u, :], pairs[:, u : 2 * P : 2], ident[:])

        def quant_vals(first, wtag, btag, copy):
            vb = tile([P, 2 * P, PACK], BF16, "vb%d" % first, btag)
            for k in range(2):
                copy(vb[:, k * P : (k + 1) * P, :].rearrange("p e t -> p (e t)").bitcast(F32).rearrange("p (e u) -> p e u", u=2),
                               turned[first + k][:].rearrange("p u e -> p e u"))
            vw = tile([P, 2 * P], U32, "vw%d" % first, wtag)
            vs = tile([P, 2 * P], U8, "vs%d" % first)
            nc.vector.quantize_mx(out=vw[:].bitcast(FP8X4), scales=vs[:], in_=vb[:].rearrange("p e t -> p (e t)"))
            return vw, vs

        gather_vals(0)
        gather_vals(1)
        gather_vals(2)
        gather_vals(3)
        vq = [quant_vals(0, None, "grp", nc.vector.tensor_copy)]
        gw = tile([P, J], U32, "gw")
        gs = tile([P, J], U8, "gs")
        for js in halves:
            nc.vector.quantize_mx(out=gw[:, js].bitcast(FP8X4), scales=gs[:, js], in_=gb[:, js, :].rearrange("p j t -> p (j t)"))
        vq.append(quant_vals(2, "gb", "vpool3", nc.scalar.copy))

        def product(e, pieces):
            vw, vs = vq[e // 2]
            cols = slice((e % 2) * P, (e % 2 + 1) * P)
            prod = bank([P, J], "prod")
            for js in pieces:
                nc.tensor.matmul_mx(out=prod[:, js], lhsT=vw[:, cols].bitcast(FP8X4), lhsT_scale=vs[:, cols],
                                    rhs=gw[:, js].bitcast(FP8X4), rhs_scale=gs[:, js], start=True, stop=True)
            return prod

        def fetch(on_vector, prod, a, b, name, tag):
            res = tile([P, b - a], F32, name, tag)
            if on_vector:
                nc.vector.tensor_copy(res[:], prod[:, a:b])
            else:
                nc.scalar.copy(res[:], prod[:, a:b])
            return res

        def put(on_vector, e, values, a, b):
            dst = win[e][:].indirect(lst4[:, a // 16 : b // 16])
            if on_vector:
                nc.vector.tensor_copy(dst, values)
            else:
                nc.scalar.activation(dst, values, COPY)

        def finish(e, tag, pieces):
            total = tile([P, M], F32, "total%d" % e, tag)
            for ms in pieces:
                nc.vector.tensor_tensor(total[:, ms], prev[e][:, ms], win[e][:, ms], ALU.add)
                nc.sync.dma_start(out[e * P : (e + 1) * P, ms], total[:, ms])

        half = J // 2
        whole = (slice(0, M),)
        res0 = fetch(False, product(0, halves), 0, J, "res0", None)
        res1 = fetch(True, product(1, halves), 0, J, "res1", "vpool3")
        put(True, 1, res1[:], 0, J)
        put(False, 0, res0[:, :half], 0, half)
        put(False, 0, res0[:, half:], half, J)
        prod2 = product(2, (slice(0, J),))
        res2s = fetch(False, prod2, 0, SHARE, "res2s", None)
        put(False, 2, res2s[:], 0, SHARE)
        res3 = fetch(False, product(3, (slice(0, J),)), 0, J, "res3", "res2s")
        put(False, 3, res3[:, :half], 0, half)
        put(False, 3, res3[:, half:], half, J)
        finish(1, None, whole)
        finish(0, "vpool3", whole)
        res2v = fetch(True, prod2, SHARE, J, "res2v", "prev1")
        put(True, 2, res2v[:], SHARE, J)
        finish(2, None, (slice(0, M // 2), slice(M // 2, M)))
        finish(3, "prev1", (slice(0, M // 2), slice(M // 2, 3 * M // 4), slice(3 * M // 4, M)))
